import numpy as np
import ml_dtypes


def mxq(x, axis, fmt="e4m3"):
    dtype, down = {"e4m3": (ml_dtypes.float8_e4m3fn, 7), "e5m2": (ml_dtypes.float8_e5m2, 14)}[fmt]
    v = np.moveaxis(np.asarray(x, np.float32).astype(ml_dtypes.bfloat16).astype(np.float64), axis, -1)
    blocks = v.reshape(v.shape[:-1] + (-1, 32))
    amax = np.abs(blocks).max(-1, keepdims=True)
    byte = np.maximum(np.where(amax > 0, np.frexp(amax)[1] - 1 + 127, 0) - down, 1)
    scale = np.exp2(byte - 127.0)
    codes = (blocks / scale).astype(np.float32).astype(dtype).astype(np.float64)
    return np.moveaxis((codes * scale).reshape(v.shape), -1, axis)


WIDE = False


def mx_kscale(k):
    if not WIDE:
        return np.ones(k)
    levels = np.array([10, -10, 5, -5, 0])
    if k % 512:
        return np.exp2(np.random.permutation(np.resize(levels, k // 32))).repeat(32)
    a = np.empty((k // 512, 16))
    for p in range(k // 512):
        a[p, :8] = np.random.permutation(np.resize(levels, 8))
        for g in range(8):
            far = levels[np.abs(levels - a[p, g]) >= 10]
            a[p, g + 8] = far[np.random.randint(len(far))]
    return np.exp2(a.ravel()).repeat(32)


def f64(x):
    return np.asarray(x).astype(np.float64)


def striped(idx):
    return np.tile(idx.reshape(-1, 16).T, (8, 1)).astype(np.uint16)


def unstriped(offs):
    return offs[:16].T.reshape(-1).astype(np.int64)


E2M1 = np.array([0.0, 0.5, 1.0, 1.5, 2.0, 3.0, 4.0, 6.0, -0.0, -0.5, -1.0, -1.5, -2.0, -3.0, -4.0, -6.0])


def pack_weight(w, fmt):
    k, n = w.shape
    w = f64(np.asarray(w, np.float32).astype(ml_dtypes.bfloat16)).reshape(k // 32, 32, n)
    amax = np.abs(w).max(1)
    if fmt == "e4m3":
        byte = np.frexp(amax)[1] - 1 + 127 - 7
    else:
        mant, ex = np.frexp(amax / 6.0)
        byte = np.where(mant > 0.5, ex, ex - 1) + 127
    byte = np.clip(np.where(amax > 0, byte, 1), 1, 254)
    scaled = (w * np.exp2(127.0 - byte)[:, None, :]).reshape(k, n).astype(np.float32)
    by_word = np.ascontiguousarray(scaled.reshape(k // 512, 128, 4, n).transpose(0, 1, 3, 2))
    if fmt == "e4m3":
        words = by_word.astype(ml_dtypes.float8_e4m3fn).view(np.uint8)
    else:
        c = by_word.astype(ml_dtypes.float4_e2m1fn).view(np.uint8) & 0xF
        words = (c[..., 0::2] | (c[..., 1::2] << 4)).reshape(k // 512, 128, 2 * n)
    return np.ascontiguousarray(words), np.ascontiguousarray(byte.astype(np.uint8).reshape(k // 512, 16, n))


def unpack_weight(words, scales, fmt):
    g, _, n = scales.shape
    words = np.ascontiguousarray(words).reshape(g, 128, n, -1)
    if fmt == "e4m3":
        vals = words.view(ml_dtypes.float8_e4m3fn).astype(np.float64)
    else:
        nib = np.empty((g, 128, n, 4), np.uint8)
        nib[..., 0::2] = words & 0xF
        nib[..., 1::2] = words >> 4
        vals = E2M1[nib]
    vals = vals * np.repeat(np.exp2(scales.astype(np.float64) - 127.0), 8, axis=1)[..., None]
    return vals.transpose(0, 1, 3, 2).reshape(g * 512, n)


def gelu(v):
    return 0.5 * v * (1.0 + np.tanh(np.sqrt(2.0 / np.pi) * (v + 0.044715 * v**3)))


def bf(x):
    return np.asarray(x, np.float32).astype(ml_dtypes.bfloat16)


def planes(Y):
    n, m = Y.shape
    b = f64(bf(Y)).reshape(n // 32, 32, m)
    amax = np.abs(b).max(1)
    byte = np.clip(np.where(amax > 0, np.frexp(amax)[1] - 1 + 127 - 7, 1), 1, 254)
    codes = (b * np.exp2(127.0 - byte)[:, None, :]).reshape(n, m).astype(np.float32).astype(ml_dtypes.float8_e4m3fn).view(np.uint8)
    words = codes.reshape(n // 512, 128, 4, m).transpose(0, 1, 3, 2)
    return np.ascontiguousarray(words), np.ascontiguousarray(byte.astype(np.uint8).reshape(n // 512, 16, m))


K, T, S, P, H, N = 1024, 2048, 1024, 512, 512, 1024

def setup_inputs():
    n = np.random.standard_normal
    s = mx_kscale(K)[:, None]
    u = mx_kscale(H)[:, None]
    tab_words, tab_scales = pack_weight(n((K, T)) * s, "e4m3")
    w1 = n((K, H)) / np.sqrt(K) / s * u.T
    b1 = 0.5 * n(H) * u[:, 0]
    w2_words, w2_scales = pack_weight(n((K, H)) / np.sqrt(K) / s * u.T, "e4m3")
    mod = np.random.uniform(0.2, 1.8, (H, S))
    wa_words, wa_scales = pack_weight(0.8 * n((H, N)) / np.sqrt(H) / u, "e2m1")
    wb = n((H, N)) / np.sqrt(H) / u
    steep = np.random.uniform(1, 3, N)
    share = np.random.uniform(0.1, 0.5, N)
    gain = 2.0 * np.exp(0.8 * n(N))
    cap = gain[:, None] * np.random.uniform(-0.1, 0.5, (N, P))
    return {"tab_words": tab_words, "tab_scales": tab_scales,
            "offs": striped(np.random.permutation(T)[:S]),
            "pos1": striped(np.random.permutation(S)[:P]),
            "pos2": striped(np.random.permutation(S)[:P]),
            "w1": w1.astype(np.float32), "b1": b1.astype(np.float32),
            "w2_words": w2_words, "w2_scales": w2_scales,
            "mod": mod.astype(np.float32),
            "wa_words": wa_words, "wa_scales": wa_scales,
            "wb": wb.astype(np.float32),
            "steep": steep.astype(np.float32), "share": share.astype(np.float32),
            "gain": gain.astype(np.float32), "cap": cap.astype(np.float32)}

def reference(tab_words, tab_scales, offs, pos1, pos2, w1, b1, w2_words, w2_scales, mod,
              wa_words, wa_scales, wb, steep, share, gain, cap):
    v = unpack_weight(tab_words, tab_scales, "e4m3")[:, unstriped(offs)]
    h = (mxq(f64(w1), 0, "e4m3").T @ v) + f64(b1)[:, None]
    f = (unpack_weight(w2_words, w2_scales, "e4m3").T @ v) * f64(mod)
    e = unpack_weight(wa_words, wa_scales, "e2m1").T @ mxq(h, 0, "e4m3")
    d = mxq(f64(wb), 0, "e4m3").T @ mxq(f, 0, "e4m3")
    top = e.max(axis=1)
    a = 1.0 / (1.0 + np.exp(-f64(steep)[:, None] * (e[:, unstriped(pos1)] - f64(share)[:, None] * top[:, None])))
    c = f64(gain)[:, None] * d[:, unstriped(pos2)]
    y = np.minimum(c * a, f64(cap))
    words, scales = planes(y)
    return y, words, scales

@@ -1,0 +1,353 @@
+from contextlib import ExitStack
+
+import concourse.mybir as mybir
+
+K, T, S, M, H, N = 1024, 2048, 1024, 512, 512, 1024
+FLOPS = 2 * (2 * K * H * S + 2 * H * N * S)
+
+F32 = mybir.dt.float32
+BF16 = mybir.dt.bfloat16
+I32 = mybir.dt.int32
+U32 = mybir.dt.uint32
+U16 = mybir.dt.uint16
+U8 = mybir.dt.uint8
+FP8X4 = mybir.dt.float8_e4m3fn_x4
+FP4X4 = mybir.dt.float4_e2m1fn_x4
+ALU = mybir.AluOpType
+ACT = mybir.ActivationFunctionType
+
+P = 128
+PACK = 4
+BANK = 512
+PASSES = K // (P * PACK)
+HALVES = S // BANK
+GROUPS = N // (P * PACK)
+QUADS = 4
+CHUNK = BANK // PACK
+
+
+def tile_list_cascade_spill_scores_kernel(
+    tc, tab_words, tab_scales, offs, pos1, pos2, w1, b1, w2_words, w2_scales, mod,
+    wa_words, wa_scales, wb, steep, share, gain, cap, out_0, out_1, out_2,
+):
+    nc = tc.nc
+    with ExitStack() as ctx:
+        keep = ctx.enter_context(tc.tile_pool(name="keep", bufs=1))
+        ring = ctx.enter_context(tc.tile_pool(name="ring", bufs=3))
+        psum = ctx.enter_context(tc.psum_pool(name="psum", bufs=4))
+
+        def kept(name, shape, dtype):
+            return keep.tile(shape, dtype, name=name, align_bytes=64)
+
+        def as_words(dram):
+            return dram.rearrange("p n i -> p (n i)").bitcast(I32)
+
+        idx = keep.tile([P, S // 16], U16, name="idx")
+        p1 = keep.tile([P, M // 16], U16, name="p1")
+        p2 = keep.tile([P, M // 16], U16, name="p2")
+        tab_w = [kept(f"tab_w{a}", [P, T], U32) for a in range(PASSES)]
+        tab_s = kept("tab_s", [P, T], U8)
+        wt_s_raw = kept("wt_s_raw", [P, N], U8)
+        w1_raw = [
+            [kept(f"w1_raw{a}{u}", [P, PACK, H // 2], F32) for u in range(2)] for a in range(PASSES)
+        ]
+        w2_raw = kept("w2_raw", [P, PASSES, H], I32)
+        wa_raw = kept("wa_raw", [P, 2 * N], U8)
+        mod_sb = [kept(f"mod{u}", [P, PACK, BANK], F32) for u in range(HALVES)]
+        wb_raw = [kept(f"wb_raw{g}", [P, PACK, BANK], F32) for g in range(GROUPS)]
+        cap_sb = [kept(f"cap{g}", [P, PACK, M], F32) for g in range(GROUPS)]
+        b1_sb = kept("b1", [P, PACK], F32)
+        steep_sb = kept("steep", [P, GROUPS, PACK], F32)
+        share_sb = kept("share", [P, GROUPS, PACK], F32)
+        gain_sb = kept("gain", [P, GROUPS, PACK], F32)
+
+        nc.vector.memset(tab_s[:].bitcast(I32), 0)
+        nc.gpsimd.memset(wt_s_raw[:].bitcast(I32), 0)
+
+        def load_weight_scales(q):
+            nc.sync.dma_start(
+                wt_s_raw[32 * q : 32 * q + 4, :].bitcast(I32),
+                wa_scales[0, 4 * q : 4 * q + 4, :].bitcast(I32),
+            )
+            nc.sync.dma_start(
+                wt_s_raw[32 * q + 4 : 32 * q + 8, :].bitcast(I32).rearrange("r (a c) -> r a c", a=PASSES),
+                w2_scales[:, 4 * q : 4 * q + 4, :].bitcast(I32).rearrange("a r c -> r a c"),
+            )
+
+        def load_w1(a):
+            rows = w1[BANK * a : BANK * (a + 1), :].rearrange("(p j) c -> p j c", j=PACK)
+            for u in range(2):
+                nc.sync.dma_start(w1_raw[a][u][:], rows[:, :, (H // 2) * u : (H // 2) * (u + 1)])
+
+        mod_rows = mod.rearrange("(p t) s -> p t s", t=PACK)
+        wb_rows = wb.rearrange("(p j) n -> p j n", j=PACK)
+        nc.sync.dma_start(tab_w[0][:].bitcast(I32), as_words(tab_words[0]))
+        nc.sync.dma_start(idx[:], offs)
+        for q in range(QUADS):
+            nc.sync.dma_start(
+                tab_s[32 * q : 32 * q + 4 * PASSES, :].bitcast(I32),
+                tab_scales[:, 4 * q : 4 * q + 4, :].bitcast(I32),
+            )
+        load_w1(0)
+        nc.sync.dma_start(tab_w[1][:].bitcast(I32), as_words(tab_words[1]))
+        nc.sync.dma_start(b1_sb[:], b1.rearrange("(p t) -> p t", t=PACK))
+        load_w1(1)
+        load_weight_scales(0)
+        nc.sync.dma_start(w2_raw[:], w2_words.rearrange("a p c i -> p a (c i)").bitcast(I32))
+        load_weight_scales(1)
+        nc.sync.dma_start(wa_raw[:].bitcast(I32), wa_words[0].bitcast(I32))
+        load_weight_scales(2)
+        nc.sync.dma_start(mod_sb[0][:], mod_rows[:, :, 0:BANK])
+        load_weight_scales(3)
+        nc.sync.dma_start(mod_sb[1][:], mod_rows[:, :, BANK:S])
+        nc.sync.dma_start(p1[:], pos1)
+        for row_sb, row in ((steep_sb, steep), (share_sb, share)):
+            nc.sync.dma_start(row_sb[:], row.rearrange("(g p t) -> p g t", p=P, t=PACK))
+        nc.sync.dma_start(wb_raw[0][:], wb_rows[:, :, 0:BANK])
+        nc.sync.dma_start(p2[:], pos2)
+        nc.sync.dma_start(gain_sb[:], gain.rearrange("(g p t) -> p g t", p=P, t=PACK))
+        nc.sync.dma_start(wb_raw[1][:], wb_rows[:, :, BANK:N])
+        for g in range(GROUPS):
+            nc.sync.dma_start(
+                cap_sb[g][:], cap[BANK * g : BANK * (g + 1), :].rearrange("(p t) m -> p t m", t=PACK)
+            )
+
+        v_w = [[kept(f"v_w{a}{u}", [P, BANK], U32) for u in range(HALVES)] for a in range(PASSES)]
+        v_s = [kept(f"v_s{u}", [P, BANK], U8) for u in range(HALVES)]
+        cols = BANK // 16
+
+        def entries(u):
+            return idx[:, cols * u : cols * (u + 1)]
+
+        def staged():
+            return ring.tile([P, PACK * BANK], BF16, name="rounded", align_bytes=64, bufs=4)
+
+        def quantised(name, rounded):
+            codes = kept(f"{name}_c", [P, BANK], U32)
+            scales = kept(f"{name}_s", [P, BANK], U8)
+            nc.vector.quantize_mx(out=codes[:].bitcast(FP8X4), scales=scales[:], in_=rounded[:])
+            return codes, scales
+
+        def round_weight(pieces):
+            rounded = staged()
+            dealt = rounded[:].rearrange("p (t m j) -> p m j t", t=PACK, j=PACK)
+            width = P // len(pieces)
+            for u, raw in enumerate(pieces):
+                nc.scalar.copy(
+                    dealt[:, width * u : width * (u + 1), :, :],
+                    raw[:].rearrange("p j (m t) -> p m j t", t=PACK),
+                )
+            return rounded
+
+        for u in range(HALVES):
+            nc.vector.tensor_copy(v_w[0][u][:], tab_w[0][:].indirect(entries(u)))
+        for u in range(HALVES):
+            nc.vector.tensor_copy(v_s[u][:], tab_s[:].indirect(entries(u)))
+        w1_q = [quantised("w10", round_weight(w1_raw[0]))]
+        for u in range(HALVES):
+            nc.vector.tensor_copy(v_w[1][u][:], tab_w[1][:].indirect(entries(u)))
+        w1_q.append(quantised("w11", round_weight(w1_raw[1])))
+
+        h_lin = []
+        for u in range(HALVES):
+            banks = [psum.tile([P, BANK], F32, name="s_bank") for t in range(PACK)]
+            order = [(a, t) for a in range(PASSES) for t in range(PACK)]
+            if u > 0:
+                order = [(a, t) for t in range(PACK) for a in range(PASSES)]
+            for a, t in order:
+                w_cols = slice(P * t, P * (t + 1))
+                nc.tensor.matmul_mx(
+                    out=banks[t][:],
+                    lhsT=w1_q[a][0][:, w_cols].bitcast(FP8X4),
+                    lhsT_scale=w1_q[a][1][:, w_cols],
+                    rhs=v_w[a][u][:].bitcast(FP8X4),
+                    rhs_scale=v_s[u][4 * a : P, :],
+                    start=(a == 0),
+                    stop=(a == PASSES - 1),
+                )
+            lin = kept(f"h_lin{u}", [P, PACK, BANK], BF16)
+            for t in range(PACK):
+                nc.scalar.activation(lin[:, t, :], banks[t][:], ACT.Identity, bias=b1_sb[:, t : t + 1])
+            h_lin.append(lin)
+
+        w2_c = kept("w2_c", [P, PASSES, H], I32)
+        wa_c = kept("wa_c", [P, 2 * N], U8)
+        wt_s = kept("wt_s", [P, N], U8)
+        nc.vector.tensor_copy(
+            w2_c[:].rearrange("p a (t m) -> p a m t", t=PACK),
+            w2_raw[:].rearrange("p a (m t) -> p a m t", t=PACK),
+        )
+        nc.vector.tensor_copy(
+            wt_s[:].rearrange("p (g t m) -> p g m t", g=GROUPS, t=PACK),
+            wt_s_raw[:].rearrange("p (g m t) -> p g m t", g=GROUPS, t=PACK),
+        )
+        nc.vector.tensor_copy(
+            wa_c[:].bitcast(U16).rearrange("p (g t m) -> p g m t", g=GROUPS, t=PACK),
+            wa_raw[:].bitcast(U16).rearrange("p (g m t) -> p g m t", g=GROUPS, t=PACK),
+        )
+
+        def h_codes(u, copy):
+            rounded = staged()
+            copy(
+                rounded[:].rearrange("p (c i t) -> p c t i", i=4, t=PACK),
+                h_lin[u][:].rearrange("p t (c i) -> p c t i", i=4),
+            )
+            return quantised(f"h{u}", rounded)
+
+        def f_codes(u):
+            rounded = staged()
+            for c in range(PACK):
+                s_cols = slice(CHUNK * c, CHUNK * (c + 1))
+                bank = psum.tile([P, PACK, CHUNK], F32, name="v_bank")
+                for t in range(PACK):
+                    for a in range(PASSES):
+                        nc.tensor.matmul_mx(
+                            out=bank[:, t, :],
+                            lhsT=w2_c[:, a, P * t : P * (t + 1)].bitcast(FP8X4),
+                            lhsT_scale=wt_s[4:P, H * a + P * t : H * a + P * (t + 1)],
+                            rhs=v_w[a][u][:, s_cols].bitcast(FP8X4),
+                            rhs_scale=v_s[u][4 * a : P, s_cols],
+                            start=(a == 0),
+                            stop=(a == PASSES - 1),
+                        )
+                nc.vector.tensor_tensor(
+                    rounded[:, BANK * c : BANK * (c + 1)].rearrange("p (c i t) -> p c t i", i=2, t=PACK),
+                    bank[:].rearrange("p t (c i) -> p c t i", i=2),
+                    mod_sb[u][:, :, s_cols].rearrange("p t (c i) -> p c t i", i=2),
+                    ALU.mult,
+                )
+            return quantised(f"f{u}", rounded)
+
+        TILES = GROUPS * PACK
+        slope = kept("slope", [P, TILES], F32)
+        shifts = kept("shifts", [P, TILES], F32)
+        tops = kept("tops", [P, TILES, HALVES], F32)
+        steep_col = steep_sb[:].rearrange("p g t -> p (g t)")
+        share_col = share_sb[:].rearrange("p g t -> p (g t)")
+        gain_col = gain_sb[:].rearrange("p g t -> p (g t)")
+        y_sb = [kept(f"y{g}", [P, PACK, M], F32) for g in range(GROUPS)]
+        y_c = [kept(f"y_c{g}", [P, M], U32) for g in range(GROUPS)]
+        y_s = [kept(f"y_s{g}", [P, M], U8) for g in range(GROUPS)]
+        out_rows = out_0.rearrange("(g p t) m -> g p t m", p=P, t=PACK)
+        e_sb, d_sb, opening, weighed, y_round = {}, {}, {}, {}, {}
+        h_q, f_q, wb_q = [], [], []
+
+        def head_scores(i, u):
+            if u == 0:
+                e_sb[i] = ring.tile([P, S], F32, name="e_sb")
+            bank = psum.tile([P, BANK], F32, name="v_bank")
+            nc.tensor.matmul_mx(
+                out=bank[:],
+                lhsT=wa_c[:, 2 * P * i : 2 * P * (i + 1)].bitcast(FP4X4),
+                lhsT_scale=wt_s[:, P * i : P * (i + 1)],
+                rhs=h_q[u][0][:].bitcast(FP8X4),
+                rhs_scale=h_q[u][1][:],
+                start=True,
+                stop=True,
+            )
+            nc.vector.tensor_scalar(
+                e_sb[i][:, BANK * u : BANK * (u + 1)], bank[:], 1.0,
+                None if u == 0 else tops[:, i, u - 1 : u], ALU.mult, ALU.max,
+                accum_out=tops[:, i, u : u + 1],
+            )
+
+        def arrival_scores(i, u):
+            g, t = divmod(i, PACK)
+            if u == 0:
+                d_sb[i] = ring.tile([P, S], F32, name="d_sb")
+            bank = psum.tile([P, BANK], F32, name="s_bank")
+            nc.tensor.matmul_mx(
+                out=bank[:],
+                lhsT=wb_q[g][0][:, P * t : P * (t + 1)].bitcast(FP8X4),
+                lhsT_scale=wb_q[g][1][:, P * t : P * (t + 1)],
+                rhs=f_q[u][0][:].bitcast(FP8X4),
+                rhs_scale=f_q[u][1][:],
+                start=True,
+                stop=True,
+            )
+            nc.scalar.copy(d_sb[i][:, BANK * u : BANK * (u + 1)], bank[:])
+
+        def shift(i):
+            nc.scalar.activation(
+                shifts[:, i : i + 1], tops[:, i, HALVES - 1 : HALVES], ACT.Copy, scale=slope[:, i : i + 1]
+            )
+
+        def look(i):
+            opening[i] = ring.tile([P, M], F32, name="opening")
+            nc.scalar.activation(
+                opening[i][:], e_sb[i][:].indirect(p1[:]), ACT.Sigmoid,
+                bias=shifts[:, i : i + 1], scale=steep_col[:, i : i + 1],
+            )
+
+        def weigh(i):
+            weighed[i] = ring.tile([P, M], F32, name="weighed")
+            nc.vector.tensor_tensor(weighed[i][:], d_sb[i][:].indirect(p2[:]), opening[i][:], ALU.mult)
+
+        def bound(i):
+            g, t = divmod(i, PACK)
+            nc.vector.scalar_tensor_tensor(
+                y_sb[g][:, t, :], weighed[i][:], gain_col[:, i : i + 1], cap_sb[g][:, t, :],
+                ALU.mult, ALU.min,
+            )
+            nc.sync.dma_start(out_rows[g, :, t, :], y_sb[g][:, t, :])
+
+        def round_y(g, lo, hi, copy):
+            if lo == 0:
+                y_round[g] = staged()
+            copy(
+                y_round[g][:, PACK * lo : PACK * hi].rearrange("p (c i t) -> p c t i", i=4, t=PACK),
+                y_sb[g][:, :, lo:hi].rearrange("p t (c i) -> p c t i", i=4),
+            )
+
+        def planes(g, lo, hi):
+            nc.vector.quantize_mx(
+                out=y_c[g][:, lo:hi].bitcast(FP8X4), scales=y_s[g][:, lo:hi],
+                in_=y_round[g][:, PACK * lo : PACK * hi],
+            )
+            nc.sync.dma_start(as_words(out_1[g])[:, lo:hi], y_c[g][:, lo:hi].bitcast(I32))
+
+        def store_scales(g):
+            for q in range(QUADS):
+                queue = nc.sync if q % 2 == 0 else nc.scalar
+                queue.dma_start(
+                    out_2[g, 4 * q : 4 * q + 4, :].bitcast(I32), y_s[g][32 * q : 32 * q + 4, :].bitcast(I32)
+                )
+
+        f_q.append(f_codes(0))
+        h_q.append(h_codes(0, nc.vector.tensor_copy))
+        h_q.append(h_codes(1, nc.scalar.copy))
+        nc.vector.scalar_tensor_tensor(slope[:], steep_col, -1.0, share_col, ALU.mult, ALU.mult)
+        wb_round = round_weight([wb_raw[0]])
+        head_scores(0, 0)
+        head_scores(0, 1)
+        f_q.append(f_codes(1))
+        wb_q.append(quantised("wb0", wb_round))
+        shift(0)
+        look(0)
+        arrival_scores(0, 0)
+        arrival_scores(0, 1)
+        head_scores(1, 0)
+        head_scores(1, 1)
+        wb_q.append(quantised("wb1", round_weight([wb_raw[1]])))
+        for i in range(TILES):
+            weigh(i)
+            if i + 1 < TILES:
+                shift(i + 1)
+                arrival_scores(i + 1, 0)
+                look(i + 1)
+                arrival_scores(i + 1, 1)
+            if i + 2 < TILES:
+                head_scores(i + 2, 0)
+            bound(i)
+            if i + 2 < TILES:
+                head_scores(i + 2, 1)
+            if PACK - 1 <= i < TILES - 1:
+                c = i - (PACK - 1)
+                round_y(0, CHUNK * c, CHUNK * (c + 1), nc.scalar.copy)
+        planes(0, 0, M)
+        store_scales(0)
+        round_y(1, 0, M // 2, nc.vector.tensor_copy)
+        round_y(1, M // 2, M, nc.scalar.copy)
+        planes(1, 0, M // 2)
+        planes(1, M // 2, M)
+        store_scales(1)

@@ -49,7 +49,7 @@ def tile_list_cascade_spill_scores_kernel(
         tab_s = kept("tab_s", [P, T], U8)
         wt_s_raw = kept("wt_s_raw", [P, N], U8)
         w1_raw = [
-            [kept(f"w1_raw{a}{u}", [P, PACK, H // 2], F32) for u in range(2)] for a in range(PASSES)
+            [kept(f"w1_raw{a}{u}", [P, PACK, H // (a + 1)], F32) for u in range(a + 1)] for a in range(PASSES)
         ]
         w2_raw = kept("w2_raw", [P, PASSES, H], I32)
         wa_raw = kept("wa_raw", [P, 2 * N], U8)
@@ -74,21 +74,26 @@ def tile_list_cascade_spill_scores_kernel(
                 w2_scales[:, 4 * q : 4 * q + 4, :].bitcast(I32).rearrange("a r c -> r a c"),
             )
 
+        def load_table_scales(a):
+            for q in range(QUADS):
+                nc.sync.dma_start(
+                    tab_s[32 * q + 4 * a : 32 * q + 4 * a + 4, :].bitcast(I32),
+                    tab_scales[a, 4 * q : 4 * q + 4, :].bitcast(I32),
+                )
+
         def load_w1(a):
             rows = w1[BANK * a : BANK * (a + 1), :].rearrange("(p j) c -> p j c", j=PACK)
-            for u in range(2):
-                nc.sync.dma_start(w1_raw[a][u][:], rows[:, :, (H // 2) * u : (H // 2) * (u + 1)])
+            width = H // len(w1_raw[a])
+            for u, raw in enumerate(w1_raw[a]):
+                nc.sync.dma_start(raw[:], rows[:, :, width * u : width * (u + 1)])
 
         mod_rows = mod.rearrange("(p t) s -> p t s", t=PACK)
         wb_rows = wb.rearrange("(p j) n -> p j n", j=PACK)
         nc.sync.dma_start(tab_w[0][:].bitcast(I32), as_words(tab_words[0]))
         nc.sync.dma_start(idx[:], offs)
-        for q in range(QUADS):
-            nc.sync.dma_start(
-                tab_s[32 * q : 32 * q + 4 * PASSES, :].bitcast(I32),
-                tab_scales[:, 4 * q : 4 * q + 4, :].bitcast(I32),
-            )
+        load_table_scales(0)
         load_w1(0)
+        load_table_scales(1)
         nc.sync.dma_start(tab_w[1][:].bitcast(I32), as_words(tab_words[1]))
         nc.sync.dma_start(b1_sb[:], b1.rearrange("(p t) -> p t", t=PACK))
         load_w1(1)
@@ -174,16 +179,16 @@ def tile_list_cascade_spill_scores_kernel(
         wa_c = kept("wa_c", [P, 2 * N], U8)
         wt_s = kept("wt_s", [P, N], U8)
         nc.vector.tensor_copy(
-            w2_c[:].rearrange("p a (t m) -> p a m t", t=PACK),
-            w2_raw[:].rearrange("p a (m t) -> p a m t", t=PACK),
+            w2_c[:].rearrange("p a (t c i) -> p a c t i", t=PACK, i=4),
+            w2_raw[:].rearrange("p a (c i t) -> p a c t i", t=PACK, i=4),
         )
         nc.vector.tensor_copy(
-            wt_s[:].rearrange("p (g t m) -> p g m t", g=GROUPS, t=PACK),
-            wt_s_raw[:].rearrange("p (g m t) -> p g m t", g=GROUPS, t=PACK),
+            wt_s[:].rearrange("p (g t c i) -> p g c t i", g=GROUPS, t=PACK, i=16),
+            wt_s_raw[:].rearrange("p (g c i t) -> p g c t i", g=GROUPS, t=PACK, i=16),
         )
         nc.vector.tensor_copy(
-            wa_c[:].bitcast(U16).rearrange("p (g t m) -> p g m t", g=GROUPS, t=PACK),
-            wa_raw[:].bitcast(U16).rearrange("p (g m t) -> p g m t", g=GROUPS, t=PACK),
+            wa_c[:].bitcast(U16).rearrange("p (g t c i) -> p g c t i", g=GROUPS, t=PACK, i=8),
+            wa_raw[:].bitcast(U16).rearrange("p (g c i t) -> p g c t i", g=GROUPS, t=PACK, i=8),
         )
 
         def h_codes(u, copy):
@@ -308,7 +313,7 @@ def tile_list_cascade_spill_scores_kernel(
 
         def store_scales(g):
             for q in range(QUADS):
-                queue = nc.sync if q % 2 == 0 else nc.scalar
+                queue = nc.scalar if g == GROUPS - 1 and q % 2 else nc.sync
                 queue.dma_start(
                     out_2[g, 4 * q : 4 * q + 4, :].bitcast(I32), y_s[g][32 * q : 32 * q + 4, :].bitcast(I32)
                 )

from contextlib import ExitStack

import concourse.mybir as mybir

K, T, S, M, H, N = 1024, 2048, 1024, 512, 512, 1024
FLOPS = 2 * (2 * K * H * S + 2 * H * N * S)

F32 = mybir.dt.float32
BF16 = mybir.dt.bfloat16
I32 = mybir.dt.int32
U32 = mybir.dt.uint32
U16 = mybir.dt.uint16
U8 = mybir.dt.uint8
FP8X4 = mybir.dt.float8_e4m3fn_x4
FP4X4 = mybir.dt.float4_e2m1fn_x4
ALU = mybir.AluOpType
ACT = mybir.ActivationFunctionType

P = 128
PACK = 4
BANK = 512
PASSES = K // (P * PACK)
HALVES = S // BANK
GROUPS = N // (P * PACK)
QUADS = 4
CHUNK = BANK // PACK


def tile_list_cascade_spill_scores_kernel(
    tc, tab_words, tab_scales, offs, pos1, pos2, w1, b1, w2_words, w2_scales, mod,
    wa_words, wa_scales, wb, steep, share, gain, cap, out_0, out_1, out_2,
):
    nc = tc.nc
    with ExitStack() as ctx:
        keep = ctx.enter_context(tc.tile_pool(name="keep", bufs=1))
        ring = ctx.enter_context(tc.tile_pool(name="ring", bufs=3))
        psum = ctx.enter_context(tc.psum_pool(name="psum", bufs=4))

        def kept(name, shape, dtype):
            return keep.tile(shape, dtype, name=name, align_bytes=64)

        def as_words(dram):
            return dram.rearrange("p n i -> p (n i)").bitcast(I32)

        idx = keep.tile([P, S // 16], U16, name="idx")
        p1 = keep.tile([P, M // 16], U16, name="p1")
        p2 = keep.tile([P, M // 16], U16, name="p2")
        tab_w = [kept(f"tab_w{a}", [P, T], U32) for a in range(PASSES)]
        tab_s = kept("tab_s", [P, T], U8)
        wt_s_raw = kept("wt_s_raw", [P, N], U8)
        w1_raw = [
            [kept(f"w1_raw{a}{u}", [P, PACK, H // (a + 1)], F32) for u in range(a + 1)] for a in range(PASSES)
        ]
        w2_raw = kept("w2_raw", [P, PASSES, H], I32)
        wa_raw = kept("wa_raw", [P, 2 * N], U8)
        mod_sb = [kept(f"mod{u}", [P, PACK, BANK], F32) for u in range(HALVES)]
        wb_raw = [kept(f"wb_raw{g}", [P, PACK, BANK], F32) for g in range(GROUPS)]
        cap_sb = [kept(f"cap{g}", [P, PACK, M], F32) for g in range(GROUPS)]
        b1_sb = kept("b1", [P, PACK], F32)
        steep_sb = kept("steep", [P, GROUPS, PACK], F32)
        share_sb = kept("share", [P, GROUPS, PACK], F32)
        gain_sb = kept("gain", [P, GROUPS, PACK], F32)

        nc.vector.memset(tab_s[:].bitcast(I32), 0)
        nc.gpsimd.memset(wt_s_raw[:].bitcast(I32), 0)

        def load_weight_scales(q):
            nc.sync.dma_start(
                wt_s_raw[32 * q : 32 * q + 4, :].bitcast(I32),
                wa_scales[0, 4 * q : 4 * q + 4, :].bitcast(I32),
            )
            nc.sync.dma_start(
                wt_s_raw[32 * q + 4 : 32 * q + 8, :].bitcast(I32).rearrange("r (a c) -> r a c", a=PASSES),
                w2_scales[:, 4 * q : 4 * q + 4, :].bitcast(I32).rearrange("a r c -> r a c"),
            )

        def load_table_scales(a):
            for q in range(QUADS):
                nc.sync.dma_start(
                    tab_s[32 * q + 4 * a : 32 * q + 4 * a + 4, :].bitcast(I32),
                    tab_scales[a, 4 * q : 4 * q + 4, :].bitcast(I32),
                )

        def load_w1(a):
            rows = w1[BANK * a : BANK * (a + 1), :].rearrange("(p j) c -> p j c", j=PACK)
            width = H // len(w1_raw[a])
            for u, raw in enumerate(w1_raw[a]):
                nc.sync.dma_start(raw[:], rows[:, :, width * u : width * (u + 1)])

        mod_rows = mod.rearrange("(p t) s -> p t s", t=PACK)
        wb_rows = wb.rearrange("(p j) n -> p j n", j=PACK)
        nc.sync.dma_start(tab_w[0][:].bitcast(I32), as_words(tab_words[0]))
        nc.sync.dma_start(idx[:], offs)
        load_table_scales(0)
        load_w1(0)
        load_table_scales(1)
        nc.sync.dma_start(tab_w[1][:].bitcast(I32), as_words(tab_words[1]))
        nc.sync.dma_start(b1_sb[:], b1.rearrange("(p t) -> p t", t=PACK))
        load_w1(1)
        load_weight_scales(0)
        nc.sync.dma_start(w2_raw[:], w2_words.rearrange("a p c i -> p a (c i)").bitcast(I32))
        load_weight_scales(1)
        nc.sync.dma_start(wa_raw[:].bitcast(I32), wa_words[0].bitcast(I32))
        load_weight_scales(2)
        nc.sync.dma_start(mod_sb[0][:], mod_rows[:, :, 0:BANK])
        load_weight_scales(3)
        nc.sync.dma_start(mod_sb[1][:], mod_rows[:, :, BANK:S])
        nc.sync.dma_start(p1[:], pos1)
        for row_sb, row in ((steep_sb, steep), (share_sb, share)):
            nc.sync.dma_start(row_sb[:], row.rearrange("(g p t) -> p g t", p=P, t=PACK))
        nc.sync.dma_start(wb_raw[0][:], wb_rows[:, :, 0:BANK])
        nc.sync.dma_start(p2[:], pos2)
        nc.sync.dma_start(gain_sb[:], gain.rearrange("(g p t) -> p g t", p=P, t=PACK))
        nc.sync.dma_start(wb_raw[1][:], wb_rows[:, :, BANK:N])
        for g in range(GROUPS):
            nc.sync.dma_start(
                cap_sb[g][:], cap[BANK * g : BANK * (g + 1), :].rearrange("(p t) m -> p t m", t=PACK)
            )

        v_w = [[kept(f"v_w{a}{u}", [P, BANK], U32) for u in range(HALVES)] for a in range(PASSES)]
        v_s = [kept(f"v_s{u}", [P, BANK], U8) for u in range(HALVES)]
        cols = BANK // 16

        def entries(u):
            return idx[:, cols * u : cols * (u + 1)]

        def staged():
            return ring.tile([P, PACK * BANK], BF16, name="rounded", align_bytes=64, bufs=4)

        def quantised(name, rounded):
            codes = kept(f"{name}_c", [P, BANK], U32)
            scales = kept(f"{name}_s", [P, BANK], U8)
            nc.vector.quantize_mx(out=codes[:].bitcast(FP8X4), scales=scales[:], in_=rounded[:])
            return codes, scales

        def round_weight(pieces):
            rounded = staged()
            dealt = rounded[:].rearrange("p (t m j) -> p m j t", t=PACK, j=PACK)
            width = P // len(pieces)
            for u, raw in enumerate(pieces):
                nc.scalar.copy(
                    dealt[:, width * u : width * (u + 1), :, :],
                    raw[:].rearrange("p j (m t) -> p m j t", t=PACK),
                )
            return rounded

        for u in range(HALVES):
            nc.vector.tensor_copy(v_w[0][u][:], tab_w[0][:].indirect(entries(u)))
        for u in range(HALVES):
            nc.vector.tensor_copy(v_s[u][:], tab_s[:].indirect(entries(u)))
        w1_q = [quantised("w10", round_weight(w1_raw[0]))]
        for u in range(HALVES):
            nc.vector.tensor_copy(v_w[1][u][:], tab_w[1][:].indirect(entries(u)))
        w1_q.append(quantised("w11", round_weight(w1_raw[1])))

        h_lin = []
        for u in range(HALVES):
            banks = [psum.tile([P, BANK], F32, name="s_bank") for t in range(PACK)]
            order = [(a, t) for a in range(PASSES) for t in range(PACK)]
            if u > 0:
                order = [(a, t) for t in range(PACK) for a in range(PASSES)]
            for a, t in order:
                w_cols = slice(P * t, P * (t + 1))
                nc.tensor.matmul_mx(
                    out=banks[t][:],
                    lhsT=w1_q[a][0][:, w_cols].bitcast(FP8X4),
                    lhsT_scale=w1_q[a][1][:, w_cols],
                    rhs=v_w[a][u][:].bitcast(FP8X4),
                    rhs_scale=v_s[u][4 * a : P, :],
                    start=(a == 0),
                    stop=(a == PASSES - 1),
                )
            lin = kept(f"h_lin{u}", [P, PACK, BANK], BF16)
            for t in range(PACK):
                nc.scalar.activation(lin[:, t, :], banks[t][:], ACT.Identity, bias=b1_sb[:, t : t + 1])
            h_lin.append(lin)

        w2_c = kept("w2_c", [P, PASSES, H], I32)
        wa_c = kept("wa_c", [P, 2 * N], U8)
        wt_s = kept("wt_s", [P, N], U8)
        nc.vector.tensor_copy(
            w2_c[:].rearrange("p a (t c i) -> p a c t i", t=PACK, i=4),
            w2_raw[:].rearrange("p a (c i t) -> p a c t i", t=PACK, i=4),
        )
        nc.vector.tensor_copy(
            wt_s[:].rearrange("p (g t c i) -> p g c t i", g=GROUPS, t=PACK, i=16),
            wt_s_raw[:].rearrange("p (g c i t) -> p g c t i", g=GROUPS, t=PACK, i=16),
        )
        nc.vector.tensor_copy(
            wa_c[:].bitcast(U16).rearrange("p (g t c i) -> p g c t i", g=GROUPS, t=PACK, i=8),
            wa_raw[:].bitcast(U16).rearrange("p (g c i t) -> p g c t i", g=GROUPS, t=PACK, i=8),
        )

        def h_codes(u, copy):
            rounded = staged()
            copy(
                rounded[:].rearrange("p (c i t) -> p c t i", i=4, t=PACK),
                h_lin[u][:].rearrange("p t (c i) -> p c t i", i=4),
            )
            return quantised(f"h{u}", rounded)

        def f_codes(u):
            rounded = staged()
            for c in range(PACK):
                s_cols = slice(CHUNK * c, CHUNK * (c + 1))
                bank = psum.tile([P, PACK, CHUNK], F32, name="v_bank")
                for t in range(PACK):
                    for a in range(PASSES):
                        nc.tensor.matmul_mx(
                            out=bank[:, t, :],
                            lhsT=w2_c[:, a, P * t : P * (t + 1)].bitcast(FP8X4),
                            lhsT_scale=wt_s[4:P, H * a + P * t : H * a + P * (t + 1)],
                            rhs=v_w[a][u][:, s_cols].bitcast(FP8X4),
                            rhs_scale=v_s[u][4 * a : P, s_cols],
                            start=(a == 0),
                            stop=(a == PASSES - 1),
                        )
                nc.vector.tensor_tensor(
                    rounded[:, BANK * c : BANK * (c + 1)].rearrange("p (c i t) -> p c t i", i=2, t=PACK),
                    bank[:].rearrange("p t (c i) -> p c t i", i=2),
                    mod_sb[u][:, :, s_cols].rearrange("p t (c i) -> p c t i", i=2),
                    ALU.mult,
                )
            return quantised(f"f{u}", rounded)

        TILES = GROUPS * PACK
        slope = kept("slope", [P, TILES], F32)
        shifts = kept("shifts", [P, TILES], F32)
        tops = kept("tops", [P, TILES, HALVES], F32)
        steep_col = steep_sb[:].rearrange("p g t -> p (g t)")
        share_col = share_sb[:].rearrange("p g t -> p (g t)")
        gain_col = gain_sb[:].rearrange("p g t -> p (g t)")
        y_sb = [kept(f"y{g}", [P, PACK, M], F32) for g in range(GROUPS)]
        y_c = [kept(f"y_c{g}", [P, M], U32) for g in range(GROUPS)]
        y_s = [kept(f"y_s{g}", [P, M], U8) for g in range(GROUPS)]
        out_rows = out_0.rearrange("(g p t) m -> g p t m", p=P, t=PACK)
        e_sb, d_sb, opening, weighed, y_round = {}, {}, {}, {}, {}
        h_q, f_q, wb_q = [], [], []

        def head_scores(i, u):
            if u == 0:
                e_sb[i] = ring.tile([P, S], F32, name="e_sb")
            bank = psum.tile([P, BANK], F32, name="v_bank")
            nc.tensor.matmul_mx(
                out=bank[:],
                lhsT=wa_c[:, 2 * P * i : 2 * P * (i + 1)].bitcast(FP4X4),
                lhsT_scale=wt_s[:, P * i : P * (i + 1)],
                rhs=h_q[u][0][:].bitcast(FP8X4),
                rhs_scale=h_q[u][1][:],
                start=True,
                stop=True,
            )
            nc.vector.tensor_scalar(
                e_sb[i][:, BANK * u : BANK * (u + 1)], bank[:], 1.0,
                None if u == 0 else tops[:, i, u - 1 : u], ALU.mult, ALU.max,
                accum_out=tops[:, i, u : u + 1],
            )

        def arrival_scores(i, u):
            g, t = divmod(i, PACK)
            if u == 0:
                d_sb[i] = ring.tile([P, S], F32, name="d_sb")
            bank = psum.tile([P, BANK], F32, name="s_bank")
            nc.tensor.matmul_mx(
                out=bank[:],
                lhsT=wb_q[g][0][:, P * t : P * (t + 1)].bitcast(FP8X4),
                lhsT_scale=wb_q[g][1][:, P * t : P * (t + 1)],
                rhs=f_q[u][0][:].bitcast(FP8X4),
                rhs_scale=f_q[u][1][:],
                start=True,
                stop=True,
            )
            nc.scalar.copy(d_sb[i][:, BANK * u : BANK * (u + 1)], bank[:])

        def shift(i):
            nc.scalar.activation(
                shifts[:, i : i + 1], tops[:, i, HALVES - 1 : HALVES], ACT.Copy, scale=slope[:, i : i + 1]
            )

        def look(i):
            opening[i] = ring.tile([P, M], F32, name="opening")
            nc.scalar.activation(
                opening[i][:], e_sb[i][:].indirect(p1[:]), ACT.Sigmoid,
                bias=shifts[:, i : i + 1], scale=steep_col[:, i : i + 1],
            )

        def weigh(i):
            weighed[i] = ring.tile([P, M], F32, name="weighed")
            nc.vector.tensor_tensor(weighed[i][:], d_sb[i][:].indirect(p2[:]), opening[i][:], ALU.mult)

        def bound(i):
            g, t = divmod(i, PACK)
            nc.vector.scalar_tensor_tensor(
                y_sb[g][:, t, :], weighed[i][:], gain_col[:, i : i + 1], cap_sb[g][:, t, :],
                ALU.mult, ALU.min,
            )
            nc.sync.dma_start(out_rows[g, :, t, :], y_sb[g][:, t, :])

        def round_y(g, lo, hi, copy):
            if lo == 0:
                y_round[g] = staged()
            copy(
                y_round[g][:, PACK * lo : PACK * hi].rearrange("p (c i t) -> p c t i", i=4, t=PACK),
                y_sb[g][:, :, lo:hi].rearrange("p t (c i) -> p c t i", i=4),
            )

        def planes(g, lo, hi):
            nc.vector.quantize_mx(
                out=y_c[g][:, lo:hi].bitcast(FP8X4), scales=y_s[g][:, lo:hi],
                in_=y_round[g][:, PACK * lo : PACK * hi],
            )
            nc.sync.dma_start(as_words(out_1[g])[:, lo:hi], y_c[g][:, lo:hi].bitcast(I32))

        def store_scales(g):
            for q in range(QUADS):
                queue = nc.scalar if g == GROUPS - 1 and q % 2 else nc.sync
                queue.dma_start(
                    out_2[g, 4 * q : 4 * q + 4, :].bitcast(I32), y_s[g][32 * q : 32 * q + 4, :].bitcast(I32)
                )

        f_q.append(f_codes(0))
        h_q.append(h_codes(0, nc.vector.tensor_copy))
        h_q.append(h_codes(1, nc.scalar.copy))
        nc.vector.scalar_tensor_tensor(slope[:], steep_col, -1.0, share_col, ALU.mult, ALU.mult)
        wb_round = round_weight([wb_raw[0]])
        head_scores(0, 0)
        head_scores(0, 1)
        f_q.append(f_codes(1))
        wb_q.append(quantised("wb0", wb_round))
        shift(0)
        look(0)
        arrival_scores(0, 0)
        arrival_scores(0, 1)
        head_scores(1, 0)
        head_scores(1, 1)
        wb_q.append(quantised("wb1", round_weight([wb_raw[1]])))
        for i in range(TILES):
            weigh(i)
            if i + 1 < TILES:
                shift(i + 1)
                arrival_scores(i + 1, 0)
                look(i + 1)
                arrival_scores(i + 1, 1)
            if i + 2 < TILES:
                head_scores(i + 2, 0)
            bound(i)
            if i + 2 < TILES:
                head_scores(i + 2, 1)
            if PACK - 1 <= i < TILES - 1:
                c = i - (PACK - 1)
                round_y(0, CHUNK * c, CHUNK * (c + 1), nc.scalar.copy)
        planes(0, 0, M)
        store_scales(0)
        round_y(1, 0, M // 2, nc.vector.tensor_copy)
        round_y(1, M // 2, M, nc.scalar.copy)
        planes(1, 0, M // 2)
        planes(1, M // 2, M)
        store_scales(1)
